import numpy as np
import ml_dtypes


def mxq(x, axis, fmt="e4m3"):
    dtype, down = {"e4m3": (ml_dtypes.float8_e4m3fn, 7), "e5m2": (ml_dtypes.float8_e5m2, 14)}[fmt]
    v = np.moveaxis(np.asarray(x, np.float32).astype(ml_dtypes.bfloat16).astype(np.float64), axis, -1)
    blocks = v.reshape(v.shape[:-1] + (-1, 32))
    amax = np.abs(blocks).max(-1, keepdims=True)
    byte = np.maximum(np.where(amax > 0, np.frexp(amax)[1] - 1 + 127, 0) - down, 1)
    scale = np.exp2(byte - 127.0)
    codes = (blocks / scale).astype(np.float32).astype(dtype).astype(np.float64)
    return np.moveaxis((codes * scale).reshape(v.shape), -1, axis)


WIDE = False


def mx_kscale(k):
    if not WIDE:
        return np.ones(k)
    levels = np.array([10, -10, 5, -5, 0])
    if k % 512:
        return np.exp2(np.random.permutation(np.resize(levels, k // 32))).repeat(32)
    a = np.empty((k // 512, 16))
    for p in range(k // 512):
        a[p, :8] = np.random.permutation(np.resize(levels, 8))
        for g in range(8):
            far = levels[np.abs(levels - a[p, g]) >= 10]
            a[p, g + 8] = far[np.random.randint(len(far))]
    return np.exp2(a.ravel()).repeat(32)


def f64(x):
    return np.asarray(x).astype(np.float64)


def striped(idx):
    return np.tile(idx.reshape(-1, 16).T, (8, 1)).astype(np.uint16)


def unstriped(offs):
    return offs[:16].T.reshape(-1).astype(np.int64)


def silu(v):
    return v / (1.0 + np.exp(-np.maximum(v, -700.0)))


K, T, E, C, N = 2048, 1024, 2, 256, 128


def by_expert(wq, xq):
    return np.concatenate([wq[e].T @ xq[:, e * C:(e + 1) * C] for e in range(E)], axis=1)


def setup_inputs():
    n = np.random.standard_normal
    s = mx_kscale(K)[:, None]
    return {
        "xT": (n((K, T)) * s).astype(np.float32),
        "w": (n((E + 1, K, N)) / np.sqrt(K) / s[None]).astype(np.float32),
        "b": (0.3 * n((N, E + 1))).astype(np.float32),
        "gate": np.tile(np.random.uniform(0.2, 1.0, E * C), (N, 1)).astype(np.float32),
        "offs": striped(np.random.permutation(T)[:E * C]),
    }


def reference(xT, w, b, gate, offs):
    idx = unstriped(offs)
    wq = mxq(f64(w), 1, "e4m3")
    xs = mxq(f64(xT), 0, "e4m3")
    ys = silu((wq[E].T @ xs) + f64(b)[:, E:])
    xq = mxq(f64(xT)[:, idx], 0, "e4m3")
    y = by_expert(wq, xq)
    y = silu(y + np.repeat(f64(b)[:, :E], C, axis=1))
    out = ys
    out[:, idx] += f64(gate) * y
    return out

@@ -1,0 +1,176 @@
+from contextlib import ExitStack
+
+import concourse.mybir as mybir
+
+K, T, E, C, N = 2048, 1024, 2, 256, 128
+S = E * C
+P = 128
+PASSES = K // 512
+FLOPS = 2 * K * N * (T + S)
+
+F32 = mybir.dt.float32
+BF16 = mybir.dt.bfloat16
+U32 = mybir.dt.uint32
+U16 = mybir.dt.uint16
+U8 = mybir.dt.uint8
+FP8X4 = mybir.dt.float8_e4m3fn_x4
+SILU = mybir.ActivationFunctionType.Silu
+MULT = mybir.AluOpType.mult
+ADD = mybir.AluOpType.add
+
+
+def tile_moe_shr_lin_silu_kernel(tc, xT, w, b, gate, offs, out):
+    nc = tc.nc
+    with ExitStack() as ctx:
+        keep = ctx.enter_context(tc.tile_pool(name="keep", bufs=1))
+        ring = ctx.enter_context(tc.tile_pool(name="ring", bufs=2))
+        psum = ctx.enter_context(tc.psum_pool(name="psum", bufs=1))
+
+        offsets = keep.tile([P, S // 16], U16, name="offsets")
+        bias = keep.tile([P, E + 1], F32, name="bias")
+        gates = keep.tile([P, S], F32, name="gates")
+        scattered = keep.tile([P, T], F32, name="scattered")
+        warm = keep.tile([P, 1], F32, name="warm")
+
+        nc.gpsimd.memset(warm[:], 0.0)
+        nc.scalar.activation(warm[:], warm[:], SILU)
+        nc.gpsimd.memset(scattered[:], 0.0)
+        nc.scalar.dma_start(out=bias[:], in_=b)
+
+        x_head = [keep.tile([P, T], F32, name="x_head_%d" % q) for q in range(4)]
+        x_raw = [None] + [[keep.tile([P, 2 * T], F32, name="x_raw_%d_%d" % (c, u)) for u in range(2)] for c in range(1, PASSES)]
+        wr_raw = [keep.tile([P, 4 * 4 * N], F32, name="wr_raw_%d" % h) for h in range(2)]
+        ws_raw = keep.tile([P, 4 * 4 * N], F32, name="ws_raw")
+
+        def load_x(c, u):
+            rows = xT[c * 512:(c + 1) * 512, :].rearrange("(p j) t -> p j t", j=4)
+            dst = x_raw[c][u][:].rearrange("p (j t) -> p j t", j=2)
+            nc.sync.dma_start(out=dst, in_=rows[:, 2 * u:2 * u + 2, :])
+
+        def load_w(dst, e, c0, passes):
+            nc.sync.dma_start(
+                out=dst.rearrange("p (c r) -> p c r", c=passes),
+                in_=w[e, c0 * 512:(c0 + passes) * 512, :].rearrange("(c p j) n -> p c (j n)", p=P, j=4),
+            )
+
+        for q in range(4):
+            rows = xT[0:512, q * 256:(q + 1) * 256].rearrange("(p j) t -> p j t", j=4)
+            nc.sync.dma_start(out=x_head[q][:].rearrange("p (j t) -> p j t", j=4), in_=rows)
+            if q == 1:
+                nc.sync.dma_start(offsets[:], offs)
+        load_x(1, 0)
+        load_x(1, 1)
+        for e in range(2):
+            load_w(wr_raw[0][:, e * 1024:(e + 1) * 1024], e, 0, 2)
+        load_x(2, 0)
+        load_x(2, 1)
+        for e in range(2):
+            load_w(wr_raw[1][:, e * 1024:(e + 1) * 1024], e, 2, 2)
+        load_x(3, 0)
+        load_x(3, 1)
+        nc.sync.dma_start(gates[:], gate)
+        load_w(ws_raw[:], 2, 0, 4)
+
+        acc_r = [psum.tile([P, C], F32, name="acc_r_%d" % e) for e in range(E)]
+        acc_s = [psum.tile([P, 512], F32, name="acc_s_%d" % h) for h in range(2)]
+        xs_codes = [keep.tile([P, T], U32, name="xs_codes_%d" % c, align_bytes=64) for c in range(PASSES)]
+        xs_scales = [keep.tile([P, T], U8, name="xs_scales_%d" % c, align_bytes=64) for c in range(PASSES)]
+        xr_codes = [keep.tile([P, S], U32, name="xr_codes_%d" % c, align_bytes=64) for c in range(PASSES)]
+        xr_scales = [keep.tile([P, S], U8, name="xr_scales_%d" % c, align_bytes=64) for c in range(PASSES)]
+        w_codes = [keep.tile([P, 512], U32, name="w_codes_%d" % i, align_bytes=64) for i in range(3)]
+        w_scales = [keep.tile([P, 512], U8, name="w_scales_%d" % i, align_bytes=64) for i in range(3)]
+
+        def planes_head(pp):
+            dst = pp[:].rearrange("p (u t j) -> p u t j", u=2, j=2)
+            for q in range(4):
+                copy = nc.scalar.copy if q < 2 else nc.vector.tensor_copy
+                copy(dst[:, :, q * 256:(q + 1) * 256, :], x_head[q][:].rearrange("p (u j t) -> p u t j", u=2, j=2))
+
+        def planes(c, u, pp):
+            src = x_raw[c][u][:].rearrange("p (j t) -> p t j", j=2)
+            dst = pp[:, u * 2048:(u + 1) * 2048].rearrange("p (t j) -> p t j", j=2)
+            nc.scalar.copy(dst, src)
+
+        def weights(i, raw):
+            grouped = ring.tile([P, 2048], BF16, name="w_grouped", align_bytes=64)
+            nc.scalar.copy(
+                grouped[:].rearrange("p (q n j) -> p q n j", q=4, j=4),
+                raw[:].rearrange("p (q j n) -> p q n j", q=4, j=4),
+            )
+            nc.vector.quantize_mx(out=w_codes[i][:].bitcast(FP8X4), scales=w_scales[i][:], in_=grouped[:])
+
+        def tokens(c):
+            pp = ring.tile([P, 4096], BF16, name="pp", align_bytes=64)
+            if c == 0:
+                planes_head(pp)
+            else:
+                planes(c, 0, pp)
+                planes(c, 1, pp)
+            g = ring.tile([P, 2048], BF16, name="g", align_bytes=64)
+            for u in range(2):
+                nc.vector.tensor_copy(
+                    g[:, u * 1024:(u + 1) * 1024].bitcast(U32),
+                    pp[:, u * 2048:(u + 1) * 2048].bitcast(U32).indirect(offsets[:]),
+                )
+            xs = ring.tile([P, 4096], BF16, name="xs", align_bytes=64)
+            xr = ring.tile([P, 2048], BF16, name="xr", align_bytes=64)
+            nc.vector.tensor_copy(
+                xs[:].rearrange("p (t u j) -> p t u j", u=2, j=2),
+                pp[:].rearrange("p (u t j) -> p t u j", u=2, j=2),
+            )
+            nc.vector.tensor_copy(
+                xr[:].rearrange("p (t u j) -> p t u j", u=2, j=2),
+                g[:].rearrange("p (u t j) -> p t u j", u=2, j=2),
+            )
+            nc.vector.quantize_mx(out=xr_codes[c][:].bitcast(FP8X4), scales=xr_scales[c][:], in_=xr[:])
+            nc.vector.quantize_mx(out=xs_codes[c][:].bitcast(FP8X4), scales=xs_scales[c][:], in_=xs[:])
+
+        def routed(c):
+            i, k = c // 2, c % 2
+            for e in range(E):
+                q = slice((e * 2 + k) * N, (e * 2 + k + 1) * N)
+                s = slice(e * C, (e + 1) * C)
+                nc.tensor.matmul_mx(
+                    out=acc_r[e][:], lhsT=w_codes[i][:, q].bitcast(FP8X4), lhsT_scale=w_scales[i][:, q],
+                    rhs=xr_codes[c][:, s].bitcast(FP8X4), rhs_scale=xr_scales[c][:, s],
+                    start=(c == 0), stop=(c == PASSES - 1),
+                )
+
+        def shared(c, h):
+            q = slice(c * N, (c + 1) * N)
+            s = slice(h * 512, (h + 1) * 512)
+            nc.tensor.matmul_mx(
+                out=acc_s[h][:], lhsT=w_codes[2][:, q].bitcast(FP8X4), lhsT_scale=w_scales[2][:, q],
+                rhs=xs_codes[c][:, s].bitcast(FP8X4), rhs_scale=xs_scales[c][:, s],
+                start=(c == 0), stop=(c == PASSES - 1),
+            )
+
+        tokens(0)
+        tokens(1)
+        weights(0, wr_raw[0])
+        routed(0)
+        routed(1)
+        tokens(2)
+        weights(1, wr_raw[1])
+        routed(2)
+        tokens(3)
+        routed(3)
+        weights(2, ws_raw)
+
+        y = keep.tile([P, S], F32, name="y")
+        for e in range(E):
+            s = slice(e * C, (e + 1) * C)
+            nc.scalar.activation(y[:, s], acc_r[e][:], SILU, bias=bias[:, e:e + 1])
+            nc.vector.tensor_tensor(
+                scattered[:].indirect(offsets[:, e * 16:(e + 1) * 16]), y[:, s], gates[:, s], MULT)
+
+        for h in range(2):
+            for c in range(PASSES):
+                shared(c, h)
+        for h in range(2):
+            s = slice(h * 512, (h + 1) * 512)
+            ys = ring.tile([P, 512], F32, name="ys")
+            res = ring.tile([P, 512], F32, name="res")
+            nc.scalar.activation(ys[:], acc_s[h][:], SILU, bias=bias[:, E:E + 1])
+            nc.vector.tensor_tensor(res[:], ys[:], scattered[:, s], ADD)
+            nc.sync.dma_start(out=out[:, s], in_=res[:])

@@ -23,7 +23,7 @@ def tile_moe_shr_lin_silu_kernel(tc, xT, w, b, gate, offs, out):
     nc = tc.nc
     with ExitStack() as ctx:
         keep = ctx.enter_context(tc.tile_pool(name="keep", bufs=1))
-        ring = ctx.enter_context(tc.tile_pool(name="ring", bufs=2))
+        ring = ctx.enter_context(tc.tile_pool(name="ring", bufs=3))
         psum = ctx.enter_context(tc.psum_pool(name="psum", bufs=1))
 
         offsets = keep.tile([P, S // 16], U16, name="offsets")
@@ -35,17 +35,16 @@ def tile_moe_shr_lin_silu_kernel(tc, xT, w, b, gate, offs, out):
         nc.gpsimd.memset(warm[:], 0.0)
         nc.scalar.activation(warm[:], warm[:], SILU)
         nc.gpsimd.memset(scattered[:], 0.0)
-        nc.scalar.dma_start(out=bias[:], in_=b)
 
-        x_head = [keep.tile([P, T], F32, name="x_head_%d" % q) for q in range(4)]
-        x_raw = [None] + [[keep.tile([P, 2 * T], F32, name="x_raw_%d_%d" % (c, u)) for u in range(2)] for c in range(1, PASSES)]
+        x_raw = [[keep.tile([P, 2 * T], F32, name="x_raw_%d_%d" % (c, u)) for u in range(2)] for c in range(PASSES)]
         wr_raw = [keep.tile([P, 4 * 4 * N], F32, name="wr_raw_%d" % h) for h in range(2)]
         ws_raw = keep.tile([P, 4 * 4 * N], F32, name="ws_raw")
 
-        def load_x(c, u):
+        def load_x(c, u, half=None):
             rows = xT[c * 512:(c + 1) * 512, :].rearrange("(p j) t -> p j t", j=4)
-            dst = x_raw[c][u][:].rearrange("p (j t) -> p j t", j=2)
-            nc.sync.dma_start(out=dst, in_=rows[:, 2 * u:2 * u + 2, :])
+            lo, step = (0, T) if half is None else (half * 512, 512)
+            dst = x_raw[c][u][:, 2 * lo:2 * (lo + step)].rearrange("p (j t) -> p j t", j=2)
+            nc.sync.dma_start(out=dst, in_=rows[:, 2 * u:2 * u + 2, lo:lo + step])
 
         def load_w(dst, e, c0, passes):
             nc.sync.dma_start(
@@ -53,21 +52,21 @@ def tile_moe_shr_lin_silu_kernel(tc, xT, w, b, gate, offs, out):
                 in_=w[e, c0 * 512:(c0 + passes) * 512, :].rearrange("(c p j) n -> p c (j n)", p=P, j=4),
             )
 
-        for q in range(4):
-            rows = xT[0:512, q * 256:(q + 1) * 256].rearrange("(p j) t -> p j t", j=4)
-            nc.sync.dma_start(out=x_head[q][:].rearrange("p (j t) -> p j t", j=4), in_=rows)
-            if q == 1:
-                nc.sync.dma_start(offsets[:], offs)
-        load_x(1, 0)
-        load_x(1, 1)
-        for e in range(2):
-            load_w(wr_raw[0][:, e * 1024:(e + 1) * 1024], e, 0, 2)
-        load_x(2, 0)
-        load_x(2, 1)
-        for e in range(2):
-            load_w(wr_raw[1][:, e * 1024:(e + 1) * 1024], e, 2, 2)
+        load_x(0, 0, 0)
+        load_x(0, 1, 0)
+        nc.sync.dma_start(offsets[:], offs)
+        nc.scalar.dma_start(out=bias[:], in_=b)
+        load_x(0, 0, 1)
+        load_x(0, 1, 1)
+        for c in range(1, 3):
+         for u in range(2):
+             load_x(c, u)
         load_x(3, 0)
+        for e in range(2):
+         load_w(wr_raw[0][:, e * 1024:(e + 1) * 1024], e, 0, 2)
         load_x(3, 1)
+        for e in range(2):
+         load_w(wr_raw[1][:, e * 1024:(e + 1) * 1024], e, 2, 2)
         nc.sync.dma_start(gates[:], gate)
         load_w(ws_raw[:], 2, 0, 4)
 
@@ -79,51 +78,55 @@ def tile_moe_shr_lin_silu_kernel(tc, xT, w, b, gate, offs, out):
         xr_scales = [keep.tile([P, S], U8, name="xr_scales_%d" % c, align_bytes=64) for c in range(PASSES)]
         w_codes = [keep.tile([P, 512], U32, name="w_codes_%d" % i, align_bytes=64) for i in range(3)]
         w_scales = [keep.tile([P, 512], U8, name="w_scales_%d" % i, align_bytes=64) for i in range(3)]
+        pp = [ring.tile([P, 4096], BF16, name="pp", align_bytes=64) for c in range(PASSES)]
+        g = [ring.tile([P, 2048], BF16, name="g", align_bytes=64) for c in range(PASSES)]
+        xs = [ring.tile([P, 4096], BF16, name="xs", align_bytes=64) for c in range(PASSES)]
+        xr = [ring.tile([P, 2048], BF16, name="xr", align_bytes=64) for c in range(PASSES)]
 
-        def planes_head(pp):
-            dst = pp[:].rearrange("p (u t j) -> p u t j", u=2, j=2)
-            for q in range(4):
-                copy = nc.scalar.copy if q < 2 else nc.vector.tensor_copy
-                copy(dst[:, :, q * 256:(q + 1) * 256, :], x_head[q][:].rearrange("p (u j t) -> p u t j", u=2, j=2))
+        def planes(c, u, engines=(nc.scalar.copy,)):
+            step = T // len(engines)
+            for i, copy in enumerate(engines):
+                if copy is None:
+                    continue
+                src = x_raw[c][u][:, i * 2 * step:(i + 1) * 2 * step].rearrange("p (j t) -> p t j", j=2)
+                lo = u * 2048 + i * 2 * step
+                copy(pp[c][:, lo:lo + 2 * step].rearrange("p (t j) -> p t j", j=2), src)
 
-        def planes(c, u, pp):
-            src = x_raw[c][u][:].rearrange("p (j t) -> p t j", j=2)
-            dst = pp[:, u * 2048:(u + 1) * 2048].rearrange("p (t j) -> p t j", j=2)
-            nc.scalar.copy(dst, src)
-
-        def weights(i, raw):
+        def group_w(i, raw, copy=nc.scalar.copy):
             grouped = ring.tile([P, 2048], BF16, name="w_grouped", align_bytes=64)
-            nc.scalar.copy(
+            copy(
                 grouped[:].rearrange("p (q n j) -> p q n j", q=4, j=4),
                 raw[:].rearrange("p (q j n) -> p q n j", q=4, j=4),
             )
+            return grouped
+
+        def quant_w(i, grouped):
             nc.vector.quantize_mx(out=w_codes[i][:].bitcast(FP8X4), scales=w_scales[i][:], in_=grouped[:])
 
-        def tokens(c):
-            pp = ring.tile([P, 4096], BF16, name="pp", align_bytes=64)
-            if c == 0:
-                planes_head(pp)
-            else:
-                planes(c, 0, pp)
-                planes(c, 1, pp)
-            g = ring.tile([P, 2048], BF16, name="g", align_bytes=64)
-            for u in range(2):
-                nc.vector.tensor_copy(
-                    g[:, u * 1024:(u + 1) * 1024].bitcast(U32),
-                    pp[:, u * 2048:(u + 1) * 2048].bitcast(U32).indirect(offsets[:]),
-                )
-            xs = ring.tile([P, 4096], BF16, name="xs", align_bytes=64)
-            xr = ring.tile([P, 2048], BF16, name="xr", align_bytes=64)
+        def gather(c, u):
             nc.vector.tensor_copy(
-                xs[:].rearrange("p (t u j) -> p t u j", u=2, j=2),
-                pp[:].rearrange("p (u t j) -> p t u j", u=2, j=2),
+                g[c][:, u * 1024:(u + 1) * 1024].bitcast(U32),
+                pp[c][:, u * 2048:(u + 1) * 2048].bitcast(U32).indirect(offsets[:]),
             )
-            nc.vector.tensor_copy(
-                xr[:].rearrange("p (t u j) -> p t u j", u=2, j=2),
-                g[:].rearrange("p (u t j) -> p t u j", u=2, j=2),
+
+        def inter_s(c, lo=0, hi=T, copy=nc.vector.tensor_copy):
+            copy(
+                xs[c][:].bitcast(F32).rearrange("p (t u) -> p t u", u=2)[:, lo:hi],
+                pp[c][:].bitcast(F32).rearrange("p (u t) -> p t u", u=2)[:, lo:hi],
             )
-            nc.vector.quantize_mx(out=xr_codes[c][:].bitcast(FP8X4), scales=xr_scales[c][:], in_=xr[:])
-            nc.vector.quantize_mx(out=xs_codes[c][:].bitcast(FP8X4), scales=xs_scales[c][:], in_=xs[:])
+
+        def inter_g(c, copy=nc.vector.tensor_copy):
+            copy(
+                xr[c][:].bitcast(F32).rearrange("p (t u) -> p t u", u=2),
+                g[c][:].bitcast(F32).rearrange("p (u t) -> p t u", u=2),
+            )
+
+        def quant_r(c):
+            nc.vector.quantize_mx(out=xr_codes[c][:].bitcast(FP8X4), scales=xr_scales[c][:], in_=xr[c][:])
+
+        def quant_s(c, lo=0, hi=T):
+            nc.vector.quantize_mx(
+                out=xs_codes[c][:, lo:hi].bitcast(FP8X4), scales=xs_scales[c][:, lo:hi], in_=xs[c][:, 4 * lo:4 * hi])
 
         def routed(c):
             i, k = c // 2, c % 2
@@ -145,32 +148,93 @@ def tile_moe_shr_lin_silu_kernel(tc, xT, w, b, gate, offs, out):
                 start=(c == 0), stop=(c == PASSES - 1),
             )
 
-        tokens(0)
-        tokens(1)
-        weights(0, wr_raw[0])
-        routed(0)
-        routed(1)
-        tokens(2)
-        weights(1, wr_raw[1])
-        routed(2)
-        tokens(3)
-        routed(3)
-        weights(2, ws_raw)
-
         y = keep.tile([P, S], F32, name="y")
-        for e in range(E):
+        ys = keep.tile([P, T], F32, name="ys")
+
+        def act_r(e):
             s = slice(e * C, (e + 1) * C)
             nc.scalar.activation(y[:, s], acc_r[e][:], SILU, bias=bias[:, e:e + 1])
+
+        def scatter(e):
+            s = slice(e * C, (e + 1) * C)
             nc.vector.tensor_tensor(
                 scattered[:].indirect(offsets[:, e * 16:(e + 1) * 16]), y[:, s], gates[:, s], MULT)
 
+        gy = keep.tile([P, S], F32, name="gy")
+
+        def gate_mul(e, eng=nc.gpsimd):
+            s = slice(e * C, (e + 1) * C)
+            eng.tensor_tensor(gy[:, s], y[:, s], gates[:, s], MULT)
+
+        def scatter_copy(e):
+            s = slice(e * C, (e + 1) * C)
+            nc.vector.tensor_copy(scattered[:].indirect(offsets[:, e * 16:(e + 1) * 16]), gy[:, s])
+
+        def act_s(lo, hi):
+            h = lo // 512
+            nc.scalar.activation(ys[:, lo:hi], acc_s[h][:, lo - 512 * h:hi - 512 * h], SILU, bias=bias[:, E:E + 1])
+
+        res = keep.tile([P, T], F32, name="res")
+
+        def finish(lo, hi):
+            nc.vector.tensor_tensor(res[:, lo:hi], ys[:, lo:hi], scattered[:, lo:hi], ADD)
+            nc.sync.dma_start(out=out[:, lo:hi], in_=res[:, lo:hi])
+
+        cs, cv = nc.scalar.copy, nc.vector.tensor_copy
+        planes(0, 0, (cs, None))
+        planes(0, 1, (cv, None))
+        inter_s(0, 0, 512)
+        planes(0, 0, (None, cs))
+        quant_s(0, 0, 512)
+        gather(0, 0)
+        planes(0, 1, (None, cs))
+        gather(0, 1)
+        planes(1, 0)
+        inter_s(0, 512, 1024)
+        inter_g(0)
+        quant_s(0, 512, 1024)
+        quant_r(0)
+        planes(1, 1)
+        gather(1, 0)
+        planes(2, 0)
+        gather(1, 1)
+        inter_s(1)
+        planes(2, 1)
+        inter_g(1)
+        quant_s(1)
+        gather(2, 0)
+        quant_r(1)
+        planes(3, 0)
+        gather(2, 1)
+        inter_s(2)
+        wg0 = group_w(0, wr_raw[0])
+        inter_g(2)
+        quant_s(2)
+        planes(3, 1)
+        gather(3, 0)
+        quant_w(0, wg0)
+        quant_r(2)
+        wg1 = group_w(1, wr_raw[1])
+        gather(3, 1)
+        routed(0)
+        routed(1)
+        inter_s(3)
+        inter_g(3)
+        wg2 = group_w(2, ws_raw)
+        quant_w(1, wg1)
+        quant_r(3)
+        routed(2)
+        routed(3)
+        quant_s(3)
+        for e in range(2):
+         act_r(e)
+        quant_w(2, wg2)
         for h in range(2):
-            for c in range(PASSES):
-                shared(c, h)
+         for c in range(PASSES):
+             shared(c, h)
+        for e in range(2):
+         scatter(e)
         for h in range(2):
-            s = slice(h * 512, (h + 1) * 512)
-            ys = ring.tile([P, 512], F32, name="ys")
-            res = ring.tile([P, 512], F32, name="res")
-            nc.scalar.activation(ys[:], acc_s[h][:], SILU, bias=bias[:, E:E + 1])
-            nc.vector.tensor_tensor(res[:], ys[:], scattered[:, s], ADD)
-            nc.sync.dma_start(out=out[:, s], in_=res[:])
+         act_s(h * 512, h * 512 + 512)
+        for h in range(2):
+         finish(h * 512, h * 512 + 512)

@@ -38,7 +38,7 @@ def tile_moe_shr_lin_silu_kernel(tc, xT, w, b, gate, offs, out):
 
         x_raw = [[keep.tile([P, 2 * T], F32, name="x_raw_%d_%d" % (c, u)) for u in range(2)] for c in range(PASSES)]
         wr_raw = [keep.tile([P, 4 * 4 * N], F32, name="wr_raw_%d" % h) for h in range(2)]
-        ws_raw = keep.tile([P, 4 * 4 * N], F32, name="ws_raw")
+        ws_raw = [keep.tile([P, 2 * 4 * N], F32, name="ws_raw_%d" % h) for h in range(2)]
 
         def load_x(c, u, half=None):
             rows = xT[c * 512:(c + 1) * 512, :].rearrange("(p j) t -> p j t", j=4)
@@ -61,14 +61,13 @@ def tile_moe_shr_lin_silu_kernel(tc, xT, w, b, gate, offs, out):
         for c in range(1, 3):
          for u in range(2):
              load_x(c, u)
-        load_x(3, 0)
-        for e in range(2):
-         load_w(wr_raw[0][:, e * 1024:(e + 1) * 1024], e, 0, 2)
-        load_x(3, 1)
-        for e in range(2):
-         load_w(wr_raw[1][:, e * 1024:(e + 1) * 1024], e, 2, 2)
+        for h in range(2):
+         for e in range(2):
+             load_w(wr_raw[h][:, e * 1024:(e + 1) * 1024], e, 2 * h, 2)
+         load_x(3, h)
+        load_w(ws_raw[0][:], 2, 0, 2)
         nc.sync.dma_start(gates[:], gate)
-        load_w(ws_raw[:], 2, 0, 4)
+        load_w(ws_raw[1][:], 2, 2, 2)
 
         acc_r = [psum.tile([P, C], F32, name="acc_r_%d" % e) for e in range(E)]
         acc_s = [psum.tile([P, 512], F32, name="acc_s_%d" % h) for h in range(2)]
@@ -76,8 +75,8 @@ def tile_moe_shr_lin_silu_kernel(tc, xT, w, b, gate, offs, out):
         xs_scales = [keep.tile([P, T], U8, name="xs_scales_%d" % c, align_bytes=64) for c in range(PASSES)]
         xr_codes = [keep.tile([P, S], U32, name="xr_codes_%d" % c, align_bytes=64) for c in range(PASSES)]
         xr_scales = [keep.tile([P, S], U8, name="xr_scales_%d" % c, align_bytes=64) for c in range(PASSES)]
-        w_codes = [keep.tile([P, 512], U32, name="w_codes_%d" % i, align_bytes=64) for i in range(3)]
-        w_scales = [keep.tile([P, 512], U8, name="w_scales_%d" % i, align_bytes=64) for i in range(3)]
+        w_codes = [keep.tile([P, 512 if i < 2 else 256], U32, name="w_codes_%d" % i, align_bytes=64) for i in range(4)]
+        w_scales = [keep.tile([P, 512 if i < 2 else 256], U8, name="w_scales_%d" % i, align_bytes=64) for i in range(4)]
         pp = [ring.tile([P, 4096], BF16, name="pp", align_bytes=64) for c in range(PASSES)]
         g = [ring.tile([P, 2048], BF16, name="g", align_bytes=64) for c in range(PASSES)]
         xs = [ring.tile([P, 4096], BF16, name="xs", align_bytes=64) for c in range(PASSES)]
@@ -92,11 +91,11 @@ def tile_moe_shr_lin_silu_kernel(tc, xT, w, b, gate, offs, out):
                 lo = u * 2048 + i * 2 * step
                 copy(pp[c][:, lo:lo + 2 * step].rearrange("p (t j) -> p t j", j=2), src)
 
-        def group_w(i, raw, copy=nc.scalar.copy):
-            grouped = ring.tile([P, 2048], BF16, name="w_grouped", align_bytes=64)
+        def group_w(raw, blocks, copy=nc.scalar.copy):
+            grouped = ring.tile([P, 512 * blocks], BF16, name="w_grouped", align_bytes=64)
             copy(
-                grouped[:].rearrange("p (q n j) -> p q n j", q=4, j=4),
-                raw[:].rearrange("p (q j n) -> p q n j", q=4, j=4),
+                grouped[:].rearrange("p (q n j) -> p q n j", q=blocks, j=4),
+                raw[:].rearrange("p (q j n) -> p q n j", q=blocks, j=4),
             )
             return grouped
 
@@ -140,10 +139,11 @@ def tile_moe_shr_lin_silu_kernel(tc, xT, w, b, gate, offs, out):
                 )
 
         def shared(c, h):
-            q = slice(c * N, (c + 1) * N)
+            i, k = 2 + c // 2, c % 2
+            q = slice(k * N, (k + 1) * N)
             s = slice(h * 512, (h + 1) * 512)
             nc.tensor.matmul_mx(
-                out=acc_s[h][:], lhsT=w_codes[2][:, q].bitcast(FP8X4), lhsT_scale=w_scales[2][:, q],
+                out=acc_s[h][:], lhsT=w_codes[i][:, q].bitcast(FP8X4), lhsT_scale=w_scales[i][:, q],
                 rhs=xs_codes[c][:, s].bitcast(FP8X4), rhs_scale=xs_scales[c][:, s],
                 start=(c == 0), stop=(c == PASSES - 1),
             )
@@ -161,6 +161,9 @@ def tile_moe_shr_lin_silu_kernel(tc, xT, w, b, gate, offs, out):
                 scattered[:].indirect(offsets[:, e * 16:(e + 1) * 16]), y[:, s], gates[:, s], MULT)
 
         gy = keep.tile([P, S], F32, name="gy")
+
+        def scatter_all():
+            nc.vector.tensor_tensor(scattered[:].indirect(offsets[:]), y[:], gates[:], MULT)
 
         def gate_mul(e, eng=nc.gpsimd):
             s = slice(e * C, (e + 1) * C)
@@ -195,45 +198,47 @@ def tile_moe_shr_lin_silu_kernel(tc, xT, w, b, gate, offs, out):
         quant_s(0, 512, 1024)
         quant_r(0)
         planes(1, 1)
-        gather(1, 0)
         planes(2, 0)
+        gather(1, 0)
+        planes(2, 1)
         gather(1, 1)
         inter_s(1)
-        planes(2, 1)
         inter_g(1)
         quant_s(1)
-        gather(2, 0)
+        wg0 = group_w(wr_raw[0], 4)
         quant_r(1)
+        gather(2, 0)
         planes(3, 0)
         gather(2, 1)
         inter_s(2)
-        wg0 = group_w(0, wr_raw[0])
+        wg1 = group_w(wr_raw[1], 4)
         inter_g(2)
         quant_s(2)
         planes(3, 1)
         gather(3, 0)
         quant_w(0, wg0)
         quant_r(2)
-        wg1 = group_w(1, wr_raw[1])
-        gather(3, 1)
         routed(0)
         routed(1)
-        inter_s(3)
-        inter_g(3)
-        wg2 = group_w(2, ws_raw)
+        gather(3, 1)
         quant_w(1, wg1)
+        inter_s(3, 0, 512)
+        inter_g(3)
+        wg2 = group_w(ws_raw[0], 2)
+        inter_s(3, 512, 1024)
         quant_r(3)
         routed(2)
         routed(3)
-        quant_s(3)
+        wg3 = group_w(ws_raw[1], 2)
         for e in range(2):
          act_r(e)
         quant_w(2, wg2)
-        for h in range(2):
-         for c in range(PASSES):
+        quant_s(3)
+        quant_w(3, wg3)
+        for c in range(PASSES):
+         for h in range(2):
              shared(c, h)
-        for e in range(2):
-         scatter(e)
+        scatter_all()
         for h in range(2):
          act_s(h * 512, h * 512 + 512)
         for h in range(2):

@@ -24,6 +24,7 @@ def tile_moe_shr_lin_silu_kernel(tc, xT, w, b, gate, offs, out):
     with ExitStack() as ctx:
         keep = ctx.enter_context(tc.tile_pool(name="keep", bufs=1))
         ring = ctx.enter_context(tc.tile_pool(name="ring", bufs=3))
+        late = ctx.enter_context(tc.tile_pool(name="late", bufs=1))
         psum = ctx.enter_context(tc.psum_pool(name="psum", bufs=1))
 
         offsets = keep.tile([P, S // 16], U16, name="offsets")
@@ -62,9 +63,9 @@ def tile_moe_shr_lin_silu_kernel(tc, xT, w, b, gate, offs, out):
          for u in range(2):
              load_x(c, u)
         for h in range(2):
+         load_x(3, h)
          for e in range(2):
              load_w(wr_raw[h][:, e * 1024:(e + 1) * 1024], e, 2 * h, 2)
-         load_x(3, h)
         load_w(ws_raw[0][:], 2, 0, 2)
         nc.sync.dma_start(gates[:], gate)
         load_w(ws_raw[1][:], 2, 2, 2)
@@ -80,6 +81,8 @@ def tile_moe_shr_lin_silu_kernel(tc, xT, w, b, gate, offs, out):
         pp = [ring.tile([P, 4096], BF16, name="pp", align_bytes=64) for c in range(PASSES)]
         g = [ring.tile([P, 2048], BF16, name="g", align_bytes=64) for c in range(PASSES)]
         xs = [ring.tile([P, 4096], BF16, name="xs", align_bytes=64) for c in range(PASSES)]
+        late_w = late.tile([P, 2048], BF16, name="late_w", tag="late", align_bytes=64)
+        late_xs = late.tile([P, 2048], BF16, name="late_xs", tag="late", align_bytes=64)
         xr = [ring.tile([P, 2048], BF16, name="xr", align_bytes=64) for c in range(PASSES)]
 
         def planes(c, u, engines=(nc.scalar.copy,)):
@@ -91,9 +94,10 @@ def tile_moe_shr_lin_silu_kernel(tc, xT, w, b, gate, offs, out):
                 lo = u * 2048 + i * 2 * step
                 copy(pp[c][:, lo:lo + 2 * step].rearrange("p (t j) -> p t j", j=2), src)
 
-        def group_w(raw, blocks, copy=nc.scalar.copy):
-            grouped = ring.tile([P, 512 * blocks], BF16, name="w_grouped", align_bytes=64)
-            copy(
+        def group_w(raw, blocks, grouped=None):
+            if grouped is None:
+                grouped = ring.tile([P, 512 * blocks], BF16, name="w_grouped", align_bytes=64)
+            nc.scalar.copy(
                 grouped[:].rearrange("p (q n j) -> p q n j", q=blocks, j=4),
                 raw[:].rearrange("p (q j n) -> p q n j", q=blocks, j=4),
             )
@@ -113,6 +117,16 @@ def tile_moe_shr_lin_silu_kernel(tc, xT, w, b, gate, offs, out):
                 xs[c][:].bitcast(F32).rearrange("p (t u) -> p t u", u=2)[:, lo:hi],
                 pp[c][:].bitcast(F32).rearrange("p (u t) -> p t u", u=2)[:, lo:hi],
             )
+
+        def inter_late():
+            nc.vector.tensor_copy(
+                late_xs[:].bitcast(F32).rearrange("p (t u) -> p t u", u=2),
+                pp[3][:].bitcast(F32).rearrange("p (u t) -> p t u", u=2)[:, 512:],
+            )
+
+        def quant_late():
+            s = slice(512, T)
+            nc.vector.quantize_mx(out=xs_codes[3][:, s].bitcast(FP8X4), scales=xs_scales[3][:, s], in_=late_xs[:])
 
         def inter_g(c, copy=nc.vector.tensor_copy):
             copy(
@@ -205,13 +219,12 @@ def tile_moe_shr_lin_silu_kernel(tc, xT, w, b, gate, offs, out):
         inter_s(1)
         inter_g(1)
         quant_s(1)
-        wg0 = group_w(wr_raw[0], 4)
         quant_r(1)
-        gather(2, 0)
         planes(3, 0)
+        gather(2, 0)
         gather(2, 1)
         inter_s(2)
-        wg1 = group_w(wr_raw[1], 4)
+        wg0 = group_w(wr_raw[0], 4)
         inter_g(2)
         quant_s(2)
         planes(3, 1)
@@ -220,20 +233,22 @@ def tile_moe_shr_lin_silu_kernel(tc, xT, w, b, gate, offs, out):
         quant_r(2)
         routed(0)
         routed(1)
+        wg1 = group_w(wr_raw[1], 4, late_w)
         gather(3, 1)
-        quant_w(1, wg1)
         inter_s(3, 0, 512)
         inter_g(3)
-        wg2 = group_w(ws_raw[0], 2)
-        inter_s(3, 512, 1024)
+        quant_s(3, 0, 512)
         quant_r(3)
+        quant_w(1, wg1)
         routed(2)
         routed(3)
+        inter_late()
+        wg2 = group_w(ws_raw[0], 2)
         wg3 = group_w(ws_raw[1], 2)
         for e in range(2):
          act_r(e)
         quant_w(2, wg2)
-        quant_s(3)
+        quant_late()
         quant_w(3, wg3)
         for c in range(PASSES):
          for h in range(2):

from contextlib import ExitStack

import concourse.mybir as mybir

K, T, E, C, N = 2048, 1024, 2, 256, 128
S = E * C
P = 128
PASSES = K // 512
FLOPS = 2 * K * N * (T + S)

F32 = mybir.dt.float32
BF16 = mybir.dt.bfloat16
U32 = mybir.dt.uint32
U16 = mybir.dt.uint16
U8 = mybir.dt.uint8
FP8X4 = mybir.dt.float8_e4m3fn_x4
SILU = mybir.ActivationFunctionType.Silu
MULT = mybir.AluOpType.mult
ADD = mybir.AluOpType.add


def tile_moe_shr_lin_silu_kernel(tc, xT, w, b, gate, offs, out):
    nc = tc.nc
    with ExitStack() as ctx:
        keep = ctx.enter_context(tc.tile_pool(name="keep", bufs=1))
        ring = ctx.enter_context(tc.tile_pool(name="ring", bufs=3))
        late = ctx.enter_context(tc.tile_pool(name="late", bufs=1))
        psum = ctx.enter_context(tc.psum_pool(name="psum", bufs=1))

        offsets = keep.tile([P, S // 16], U16, name="offsets")
        bias = keep.tile([P, E + 1], F32, name="bias")
        gates = keep.tile([P, S], F32, name="gates")
        scattered = keep.tile([P, T], F32, name="scattered")
        warm = keep.tile([P, 1], F32, name="warm")

        nc.gpsimd.memset(warm[:], 0.0)
        nc.scalar.activation(warm[:], warm[:], SILU)
        nc.gpsimd.memset(scattered[:], 0.0)

        x_raw = [[keep.tile([P, 2 * T], F32, name="x_raw_%d_%d" % (c, u)) for u in range(2)] for c in range(PASSES)]
        wr_raw = [keep.tile([P, 4 * 4 * N], F32, name="wr_raw_%d" % h) for h in range(2)]
        ws_raw = [keep.tile([P, 2 * 4 * N], F32, name="ws_raw_%d" % h) for h in range(2)]

        def load_x(c, u, half=None):
            rows = xT[c * 512:(c + 1) * 512, :].rearrange("(p j) t -> p j t", j=4)
            lo, step = (0, T) if half is None else (half * 512, 512)
            dst = x_raw[c][u][:, 2 * lo:2 * (lo + step)].rearrange("p (j t) -> p j t", j=2)
            nc.sync.dma_start(out=dst, in_=rows[:, 2 * u:2 * u + 2, lo:lo + step])

        def load_w(dst, e, c0, passes):
            nc.sync.dma_start(
                out=dst.rearrange("p (c r) -> p c r", c=passes),
                in_=w[e, c0 * 512:(c0 + passes) * 512, :].rearrange("(c p j) n -> p c (j n)", p=P, j=4),
            )

        load_x(0, 0, 0)
        load_x(0, 1, 0)
        nc.sync.dma_start(offsets[:], offs)
        nc.scalar.dma_start(out=bias[:], in_=b)
        load_x(0, 0, 1)
        load_x(0, 1, 1)
        for c in range(1, 3):
         for u in range(2):
             load_x(c, u)
        for h in range(2):
         load_x(3, h)
         for e in range(2):
             load_w(wr_raw[h][:, e * 1024:(e + 1) * 1024], e, 2 * h, 2)
        load_w(ws_raw[0][:], 2, 0, 2)
        nc.sync.dma_start(gates[:], gate)
        load_w(ws_raw[1][:], 2, 2, 2)

        acc_r = [psum.tile([P, C], F32, name="acc_r_%d" % e) for e in range(E)]
        acc_s = [psum.tile([P, 512], F32, name="acc_s_%d" % h) for h in range(2)]
        xs_codes = [keep.tile([P, T], U32, name="xs_codes_%d" % c, align_bytes=64) for c in range(PASSES)]
        xs_scales = [keep.tile([P, T], U8, name="xs_scales_%d" % c, align_bytes=64) for c in range(PASSES)]
        xr_codes = [keep.tile([P, S], U32, name="xr_codes_%d" % c, align_bytes=64) for c in range(PASSES)]
        xr_scales = [keep.tile([P, S], U8, name="xr_scales_%d" % c, align_bytes=64) for c in range(PASSES)]
        w_codes = [keep.tile([P, 512 if i < 2 else 256], U32, name="w_codes_%d" % i, align_bytes=64) for i in range(4)]
        w_scales = [keep.tile([P, 512 if i < 2 else 256], U8, name="w_scales_%d" % i, align_bytes=64) for i in range(4)]
        pp = [ring.tile([P, 4096], BF16, name="pp", align_bytes=64) for c in range(PASSES)]
        g = [ring.tile([P, 2048], BF16, name="g", align_bytes=64) for c in range(PASSES)]
        xs = [ring.tile([P, 4096], BF16, name="xs", align_bytes=64) for c in range(PASSES)]
        late_w = late.tile([P, 2048], BF16, name="late_w", tag="late", align_bytes=64)
        late_xs = late.tile([P, 2048], BF16, name="late_xs", tag="late", align_bytes=64)
        xr = [ring.tile([P, 2048], BF16, name="xr", align_bytes=64) for c in range(PASSES)]

        def planes(c, u, engines=(nc.scalar.copy,)):
            step = T // len(engines)
            for i, copy in enumerate(engines):
                if copy is None:
                    continue
                src = x_raw[c][u][:, i * 2 * step:(i + 1) * 2 * step].rearrange("p (j t) -> p t j", j=2)
                lo = u * 2048 + i * 2 * step
                copy(pp[c][:, lo:lo + 2 * step].rearrange("p (t j) -> p t j", j=2), src)

        def group_w(raw, blocks, grouped=None):
            if grouped is None:
                grouped = ring.tile([P, 512 * blocks], BF16, name="w_grouped", align_bytes=64)
            nc.scalar.copy(
                grouped[:].rearrange("p (q n j) -> p q n j", q=blocks, j=4),
                raw[:].rearrange("p (q j n) -> p q n j", q=blocks, j=4),
            )
            return grouped

        def quant_w(i, grouped):
            nc.vector.quantize_mx(out=w_codes[i][:].bitcast(FP8X4), scales=w_scales[i][:], in_=grouped[:])

        def gather(c, u):
            nc.vector.tensor_copy(
                g[c][:, u * 1024:(u + 1) * 1024].bitcast(U32),
                pp[c][:, u * 2048:(u + 1) * 2048].bitcast(U32).indirect(offsets[:]),
            )

        def inter_s(c, lo=0, hi=T, copy=nc.vector.tensor_copy):
            copy(
                xs[c][:].bitcast(F32).rearrange("p (t u) -> p t u", u=2)[:, lo:hi],
                pp[c][:].bitcast(F32).rearrange("p (u t) -> p t u", u=2)[:, lo:hi],
            )

        def inter_late():
            nc.vector.tensor_copy(
                late_xs[:].bitcast(F32).rearrange("p (t u) -> p t u", u=2),
                pp[3][:].bitcast(F32).rearrange("p (u t) -> p t u", u=2)[:, 512:],
            )

        def quant_late():
            s = slice(512, T)
            nc.vector.quantize_mx(out=xs_codes[3][:, s].bitcast(FP8X4), scales=xs_scales[3][:, s], in_=late_xs[:])

        def inter_g(c, copy=nc.vector.tensor_copy):
            copy(
                xr[c][:].bitcast(F32).rearrange("p (t u) -> p t u", u=2),
                g[c][:].bitcast(F32).rearrange("p (u t) -> p t u", u=2),
            )

        def quant_r(c):
            nc.vector.quantize_mx(out=xr_codes[c][:].bitcast(FP8X4), scales=xr_scales[c][:], in_=xr[c][:])

        def quant_s(c, lo=0, hi=T):
            nc.vector.quantize_mx(
                out=xs_codes[c][:, lo:hi].bitcast(FP8X4), scales=xs_scales[c][:, lo:hi], in_=xs[c][:, 4 * lo:4 * hi])

        def routed(c):
            i, k = c // 2, c % 2
            for e in range(E):
                q = slice((e * 2 + k) * N, (e * 2 + k + 1) * N)
                s = slice(e * C, (e + 1) * C)
                nc.tensor.matmul_mx(
                    out=acc_r[e][:], lhsT=w_codes[i][:, q].bitcast(FP8X4), lhsT_scale=w_scales[i][:, q],
                    rhs=xr_codes[c][:, s].bitcast(FP8X4), rhs_scale=xr_scales[c][:, s],
                    start=(c == 0), stop=(c == PASSES - 1),
                )

        def shared(c, h):
            i, k = 2 + c // 2, c % 2
            q = slice(k * N, (k + 1) * N)
            s = slice(h * 512, (h + 1) * 512)
            nc.tensor.matmul_mx(
                out=acc_s[h][:], lhsT=w_codes[i][:, q].bitcast(FP8X4), lhsT_scale=w_scales[i][:, q],
                rhs=xs_codes[c][:, s].bitcast(FP8X4), rhs_scale=xs_scales[c][:, s],
                start=(c == 0), stop=(c == PASSES - 1),
            )

        y = keep.tile([P, S], F32, name="y")
        ys = keep.tile([P, T], F32, name="ys")

        def act_r(e):
            s = slice(e * C, (e + 1) * C)
            nc.scalar.activation(y[:, s], acc_r[e][:], SILU, bias=bias[:, e:e + 1])

        def scatter(e):
            s = slice(e * C, (e + 1) * C)
            nc.vector.tensor_tensor(
                scattered[:].indirect(offsets[:, e * 16:(e + 1) * 16]), y[:, s], gates[:, s], MULT)

        gy = keep.tile([P, S], F32, name="gy")

        def scatter_all():
            nc.vector.tensor_tensor(scattered[:].indirect(offsets[:]), y[:], gates[:], MULT)

        def gate_mul(e, eng=nc.gpsimd):
            s = slice(e * C, (e + 1) * C)
            eng.tensor_tensor(gy[:, s], y[:, s], gates[:, s], MULT)

        def scatter_copy(e):
            s = slice(e * C, (e + 1) * C)
            nc.vector.tensor_copy(scattered[:].indirect(offsets[:, e * 16:(e + 1) * 16]), gy[:, s])

        def act_s(lo, hi):
            h = lo // 512
            nc.scalar.activation(ys[:, lo:hi], acc_s[h][:, lo - 512 * h:hi - 512 * h], SILU, bias=bias[:, E:E + 1])

        res = keep.tile([P, T], F32, name="res")

        def finish(lo, hi):
            nc.vector.tensor_tensor(res[:, lo:hi], ys[:, lo:hi], scattered[:, lo:hi], ADD)
            nc.sync.dma_start(out=out[:, lo:hi], in_=res[:, lo:hi])

        cs, cv = nc.scalar.copy, nc.vector.tensor_copy
        planes(0, 0, (cs, None))
        planes(0, 1, (cv, None))
        inter_s(0, 0, 512)
        planes(0, 0, (None, cs))
        quant_s(0, 0, 512)
        gather(0, 0)
        planes(0, 1, (None, cs))
        gather(0, 1)
        planes(1, 0)
        inter_s(0, 512, 1024)
        inter_g(0)
        quant_s(0, 512, 1024)
        quant_r(0)
        planes(1, 1)
        planes(2, 0)
        gather(1, 0)
        planes(2, 1)
        gather(1, 1)
        inter_s(1)
        inter_g(1)
        quant_s(1)
        quant_r(1)
        planes(3, 0)
        gather(2, 0)
        gather(2, 1)
        inter_s(2)
        wg0 = group_w(wr_raw[0], 4)
        inter_g(2)
        quant_s(2)
        planes(3, 1)
        gather(3, 0)
        quant_w(0, wg0)
        quant_r(2)
        routed(0)
        routed(1)
        wg1 = group_w(wr_raw[1], 4, late_w)
        gather(3, 1)
        inter_s(3, 0, 512)
        inter_g(3)
        quant_s(3, 0, 512)
        quant_r(3)
        quant_w(1, wg1)
        routed(2)
        routed(3)
        inter_late()
        wg2 = group_w(ws_raw[0], 2)
        wg3 = group_w(ws_raw[1], 2)
        for e in range(2):
         act_r(e)
        quant_w(2, wg2)
        quant_late()
        quant_w(3, wg3)
        for c in range(PASSES):
         for h in range(2):
             shared(c, h)
        scatter_all()
        for h in range(2):
         act_s(h * 512, h * 512 + 512)
        for h in range(2):
         finish(h * 512, h * 512 + 512)
